import numpy as np
import ml_dtypes


def mxq(x, axis, fmt="e4m3"):
    dtype, down = {"e4m3": (ml_dtypes.float8_e4m3fn, 7), "e5m2": (ml_dtypes.float8_e5m2, 14)}[fmt]
    v = np.moveaxis(np.asarray(x, np.float32).astype(ml_dtypes.bfloat16).astype(np.float64), axis, -1)
    blocks = v.reshape(v.shape[:-1] + (-1, 32))
    amax = np.abs(blocks).max(-1, keepdims=True)
    byte = np.maximum(np.where(amax > 0, np.frexp(amax)[1] - 1 + 127, 0) - down, 1)
    scale = np.exp2(byte - 127.0)
    codes = (blocks / scale).astype(np.float32).astype(dtype).astype(np.float64)
    return np.moveaxis((codes * scale).reshape(v.shape), -1, axis)


WIDE = False


def mx_kscale(k):
    if not WIDE:
        return np.ones(k)
    levels = np.array([10, -10, 5, -5, 0])
    if k % 512:
        return np.exp2(np.random.permutation(np.resize(levels, k // 32))).repeat(32)
    a = np.empty((k // 512, 16))
    for p in range(k // 512):
        a[p, :8] = np.random.permutation(np.resize(levels, 8))
        for g in range(8):
            far = levels[np.abs(levels - a[p, g]) >= 10]
            a[p, g + 8] = far[np.random.randint(len(far))]
    return np.exp2(a.ravel()).repeat(32)


def f64(x):
    return np.asarray(x).astype(np.float64)


def striped(idx):
    return np.tile(idx.reshape(-1, 16).T, (8, 1)).astype(np.uint16)


def unstriped(offs):
    return offs[:16].T.reshape(-1).astype(np.int64)


def pack_weight(w):
    k, n = w.shape
    w = f64(np.asarray(w, np.float32).astype(ml_dtypes.bfloat16)).reshape(k // 32, 32, n)
    amax = np.abs(w).max(1)
    byte = np.clip(np.where(amax > 0, np.frexp(amax)[1] - 1 + 127 - 7, 1), 1, 254)
    scaled = (w * np.exp2(127.0 - byte)[:, None, :]).reshape(k, n).astype(np.float32)
    words = np.ascontiguousarray(scaled.reshape(k // 512, 128, 4, n).transpose(0, 1, 3, 2)).astype(ml_dtypes.float8_e4m3fn).view(np.uint8)
    return words, np.ascontiguousarray(byte.astype(np.uint8).reshape(k // 512, 16, n))


def unpack_weight(words, scales):
    g, p, n, _ = words.shape
    vals = np.ascontiguousarray(words).view(ml_dtypes.float8_e4m3fn).astype(np.float64) * np.repeat(np.exp2(scales.astype(np.float64) - 127.0), 8, axis=1)[..., None]
    return vals.transpose(0, 1, 3, 2).reshape(g * 512, n)


K, T, S, N, H, U = 512, 1024, 512, 128, 512, 1024


def setup_inputs():
    n = np.random.standard_normal
    s = mx_kscale(K)[:, None]
    u = mx_kscale(H)
    packed_xT = pack_weight(n((K, T)) * s)
    return {
        "x_words": packed_xT[0],
        "x_scales": packed_xT[1],
        "w1": (n((K, H)) / np.sqrt(K) / s).astype(np.float32),
        "w2": (n((K, H)) / np.sqrt(K) / s).astype(np.float32),
        "unit": (np.random.uniform(0.6, 1.4, (H, 1)) * u[:, None]).astype(np.float32),
        "w3": (n((H, N)) / np.sqrt(H) / u[:, None]).astype(np.float32),
        "offs": striped(np.random.permutation(T)[:S]),
        "va": striped(np.random.permutation(np.concatenate([np.arange(S), np.random.randint(0, S, U - S)]))),
        "vb": striped(np.random.permutation(np.concatenate([np.arange(S), np.random.randint(0, S, U - S)]))),
        "vc": striped(np.random.permutation(np.concatenate([np.arange(S), np.random.randint(0, S, U - S)]))),
        "tr": striped(np.random.permutation(np.concatenate([np.arange(S), np.random.randint(0, S, U - S)]))),
    }


def reference(x_words, x_scales, w1, w2, unit, w3, offs, va, vb, vc, tr):
    xq = unpack_weight(x_words, x_scales)[:, unstriped(offs)]
    y = mxq(f64(w1), 0, "e4m3").T @ xq
    yva = y[:, unstriped(va)]
    yvb = y[:, unstriped(vb)]
    yvc = y[:, unstriped(vc)]
    vote = yva + yvb + yvc
    z1 = mxq(f64(w2), 0, "e4m3").T @ xq
    zt = z1[:, unstriped(tr)]
    yt = y[:, unstriped(tr)]
    hid = f64(unit) * (vote * zt + 0.5 * yt)
    return mxq(f64(w3), 0, "e4m3").T @ mxq(hid, 0, "e4m3")

@@ -1,0 +1,170 @@
+from contextlib import ExitStack
+
+import concourse.mybir as mybir
+
+K, T, S, N, H, U = 512, 1024, 512, 128, 512, 1024
+FLOPS = 2 * K * H * S * 2 + 2 * H * N * U
+
+F32 = mybir.dt.float32
+BF16 = mybir.dt.bfloat16
+I32 = mybir.dt.int32
+U32 = mybir.dt.uint32
+U16 = mybir.dt.uint16
+U8 = mybir.dt.uint8
+FP8X4 = mybir.dt.float8_e4m3fn_x4
+ADD, MULT = mybir.AluOpType.add, mybir.AluOpType.mult
+COPY = mybir.ActivationFunctionType.Copy
+
+P = 128
+PACK = 4
+LANES = 16
+CHUNKS = ((0, 384), (384, 384), (768, 256))
+FUSED_VB = ((0, 0), (0, 1))
+
+
+def tile_picked_yvotepr_tru_p_kernel(tc, x_words, x_scales, w1, w2, unit, w3, offs, va, vb, vc, tr, out):
+    nc = tc.nc
+    with ExitStack() as ctx:
+        lists = ctx.enter_context(tc.tile_pool(name="lists", bufs=1))
+        keep = ctx.enter_context(tc.tile_pool(name="keep", bufs=1))
+        work = ctx.enter_context(tc.tile_pool(name="work", bufs=4))
+        items = ctx.enter_context(tc.tile_pool(name="items", bufs=2))
+        first_psum = ctx.enter_context(tc.psum_pool(name="first_psum", bufs=4))
+        last_psum = ctx.enter_context(tc.psum_pool(name="last_psum", bufs=2))
+
+        def load_list(name, src):
+            tile = lists.tile([P, src.shape[1]], U16, name=name)
+            nc.sync.dma_start(tile[:], src)
+            return tile
+
+        def load_rows(name, w):
+            raw = keep.tile([P, PACK, w.shape[1]], F32, name=name)
+            nc.sync.dma_start(raw[:], w.rearrange("(p j) c -> p j c", j=PACK))
+            return raw
+
+        table_scales = keep.tile([P, T], U8, name="table_scales")
+        nc.vector.memset(table_scales[:].bitcast(I32), 0)
+        for q in range(4):
+            nc.scalar.dma_start(
+                table_scales[32 * q : 32 * q + 4, :].bitcast(I32),
+                x_scales[0, 4 * q : 4 * q + 4, :].bitcast(I32),
+            )
+        offs_sb = load_list("offs_sb", offs)
+        table_words = keep.tile([P, T], I32, name="table_words")
+        nc.sync.dma_start(table_words[:], x_words[0].rearrange("p n r -> p (n r)").bitcast(I32))
+        w1_raw = load_rows("w1_raw", w1)
+        unit_sb = keep.tile([P, PACK], F32, name="unit_sb")
+        nc.sync.dma_start(unit_sb[:], unit.rearrange("(p t) o -> p (t o)", t=PACK))
+        va_sb = load_list("va_sb", va)
+        w2_raw = load_rows("w2_raw", w2)
+        vb_sb = load_list("vb_sb", vb)
+        vc_sb = load_list("vc_sb", vc)
+        tr_sb = load_list("tr_sb", tr)
+        w3_raw = load_rows("w3_raw", w3)
+
+        half_unit = keep.tile([P, PACK], F32, name="half_unit")
+        nc.scalar.activation(half_unit[:], unit_sb[:], COPY, scale=0.5)
+
+        x_codes = keep.tile([P, S], U32, name="x_codes", align_bytes=64)
+        x_bytes = keep.tile([P, S], U8, name="x_bytes", align_bytes=64)
+        nc.vector.tensor_copy(x_bytes[:], table_scales[:].indirect(offs_sb[:]))
+        nc.vector.tensor_copy(x_codes[:], table_words[:].bitcast(U32).indirect(offs_sb[:]))
+
+        def round_pair(name, raw, pair):
+            grouped = keep.tile([P, 2 * P * PACK], BF16, name=name, align_bytes=64)
+            nc.vector.tensor_copy(
+                grouped[:].rearrange("p (e m j) -> p m j e", e=2, j=PACK),
+                raw[:].rearrange("p j (m t) -> p m j t", t=PACK)[:, :, :, 2 * pair : 2 * pair + 2],
+            )
+            return grouped
+
+        def quantize(pool, name, grouped, width):
+            codes = pool.tile([P, width], U32, name=name + "_codes", align_bytes=64)
+            scales = pool.tile([P, width], U8, name=name + "_scales", align_bytes=64)
+            nc.vector.quantize_mx(out=codes[:].bitcast(FP8X4), scales=scales[:], in_=grouped)
+            return codes, scales
+
+        def project(name, weights, t, scale):
+            codes, scales = weights[t // 2]
+            cols = slice(P * (t % 2), P * (t % 2 + 1))
+            bank = first_psum.tile([P, S], F32, name="bank")
+            nc.tensor.matmul_mx(
+                out=bank[:],
+                lhsT=codes[:, cols].bitcast(FP8X4),
+                lhsT_scale=scales[:, cols],
+                rhs=x_codes[:].bitcast(FP8X4),
+                rhs_scale=x_bytes[:],
+                start=True,
+                stop=True,
+            )
+            window = keep.tile([P, S], F32, name=name)
+            nc.scalar.activation(window[:], bank[:], COPY, scale=scale)
+            return window
+
+        w1_bf = [round_pair("w1_bf%d" % e, w1_raw, e) for e in range(2)]
+        w1_mx = [quantize(keep, "w1_%d" % e, w1_bf[e][:], 2 * P) for e in range(2)]
+        w2_bf = [round_pair("w2_bf%d" % e, w2_raw, e) for e in range(2)]
+        w2_mx = [quantize(keep, "w2_%d" % e, w2_bf[e][:], 2 * P) for e in range(2)]
+        w3_bf = keep.tile([P, N * PACK], BF16, name="w3_bf", align_bytes=64)
+        nc.vector.tensor_copy(
+            w3_bf[:].rearrange("p (c e j) -> p c j e", e=2, j=PACK),
+            w3_raw[:].rearrange("p j (c e) -> p c j e", e=2),
+        )
+        w3_codes, w3_scales = quantize(keep, "w3", w3_bf[:], N)
+
+        y_win, z_win = {}, {}
+        for c, (r0, n) in enumerate(CHUNKS):
+            cols = slice(r0 // LANES, (r0 + n) // LANES)
+            judged = items.tile([P, PACK, n], F32, name="judged")
+            own = items.tile([P, PACK, n], F32, name="own")
+            for pair in range(2):
+                ts = (2 * pair, 2 * pair + 1)
+                a, b, ab, abc = {}, {}, {}, {}
+                for t in ts:
+                    if c == 0:
+                        y_win[t] = project("y%d" % t, w1_mx, t, half_unit[:, t : t + 1])
+                    a[t] = work.tile([P, n], F32, name="a")
+                    nc.scalar.activation(a[t][:], y_win[t][:].indirect(va_sb[:, cols]), COPY)
+                    if (c, t) not in FUSED_VB:
+                        b[t] = work.tile([P, n], F32, name="b")
+                        nc.scalar.activation(b[t][:], y_win[t][:].indirect(vb_sb[:, cols]), COPY)
+                for t in ts:
+                    if c == 0:
+                        z_win[t] = project("z%d" % t, w2_mx, t, 2.0)
+                for t in ts:
+                    nc.scalar.activation(own[:, t, :], y_win[t][:].indirect(tr_sb[:, cols]), COPY)
+                for t in ts:
+                    ab[t] = work.tile([P, n], F32, name="ab")
+                    if (c, t) in FUSED_VB:
+                        nc.vector.tensor_tensor(ab[t][:], y_win[t][:].indirect(vb_sb[:, cols]), a[t][:], ADD)
+                    else:
+                        nc.vector.tensor_tensor(ab[t][:], b[t][:], a[t][:], ADD)
+                for t in ts:
+                    abc[t] = work.tile([P, n], F32, name="abc")
+                    nc.vector.tensor_tensor(abc[t][:], y_win[t][:].indirect(vc_sb[:, cols]), ab[t][:], ADD)
+                for t in ts:
+                    nc.vector.tensor_tensor(judged[:, t, :], z_win[t][:].indirect(tr_sb[:, cols]), abc[t][:], MULT)
+
+            hid = items.tile([P, n * PACK], BF16, name="hid", align_bytes=64)
+            nc.vector.tensor_tensor(
+                hid[:].rearrange("p (c e t) -> p c t e", e=2, t=PACK),
+                judged[:].rearrange("p t (c e) -> p c t e", e=2),
+                own[:].rearrange("p t (c e) -> p c t e", e=2),
+                ADD,
+            )
+            hid_codes, hid_scales = quantize(items, "hid", hid[:], n)
+            acc = last_psum.tile([P, n], F32, name="acc")
+            for n0 in range(0, n, 256):
+                part = slice(n0, min(n0 + 256, n))
+                nc.tensor.matmul_mx(
+                    out=acc[:, part],
+                    lhsT=w3_codes[:].bitcast(FP8X4),
+                    lhsT_scale=w3_scales[:],
+                    rhs=hid_codes[:, part].bitcast(FP8X4),
+                    rhs_scale=hid_scales[:, part],
+                    start=True,
+                    stop=True,
+                )
+            result = items.tile([P, n], F32, name="result")
+            nc.scalar.activation(result[:], acc[:], COPY)
+            nc.sync.dma_start(out[:, r0 : r0 + n], result[:])

@@ -19,7 +19,6 @@ P = 128
 PACK = 4
 LANES = 16
 CHUNKS = ((0, 384), (384, 384), (768, 256))
-FUSED_VB = ((0, 0), (0, 1))
 
 
 def tile_picked_yvotepr_tru_p_kernel(tc, x_words, x_scales, w1, w2, unit, w3, offs, va, vb, vc, tr, out):
@@ -27,10 +26,10 @@ def tile_picked_yvotepr_tru_p_kernel(tc, x_words, x_scales, w1, w2, unit, w3, of
     with ExitStack() as ctx:
         lists = ctx.enter_context(tc.tile_pool(name="lists", bufs=1))
         keep = ctx.enter_context(tc.tile_pool(name="keep", bufs=1))
-        work = ctx.enter_context(tc.tile_pool(name="work", bufs=4))
-        items = ctx.enter_context(tc.tile_pool(name="items", bufs=2))
+        work = ctx.enter_context(tc.tile_pool(name="work", bufs=8))
+        items = ctx.enter_context(tc.tile_pool(name="items", bufs=3))
         first_psum = ctx.enter_context(tc.psum_pool(name="first_psum", bufs=4))
-        last_psum = ctx.enter_context(tc.psum_pool(name="last_psum", bufs=2))
+        last_psum = ctx.enter_context(tc.psum_pool(name="last_psum", bufs=4))
 
         def load_list(name, src):
             tile = lists.tile([P, src.shape[1]], U16, name=name)
@@ -43,15 +42,15 @@ def tile_picked_yvotepr_tru_p_kernel(tc, x_words, x_scales, w1, w2, unit, w3, of
             return raw
 
         table_scales = keep.tile([P, T], U8, name="table_scales")
-        nc.vector.memset(table_scales[:].bitcast(I32), 0)
-        for q in range(4):
-            nc.scalar.dma_start(
-                table_scales[32 * q : 32 * q + 4, :].bitcast(I32),
-                x_scales[0, 4 * q : 4 * q + 4, :].bitcast(I32),
-            )
+        nc.gpsimd.memset(table_scales[:].bitcast(I32), 0)
         offs_sb = load_list("offs_sb", offs)
         table_words = keep.tile([P, T], I32, name="table_words")
         nc.sync.dma_start(table_words[:], x_words[0].rearrange("p n r -> p (n r)").bitcast(I32))
+        for q in range(4):
+            nc.sync.dma_start(
+                table_scales[32 * q : 32 * q + 4, :].bitcast(I32),
+                x_scales[0, 4 * q : 4 * q + 4, :].bitcast(I32),
+            )
         w1_raw = load_rows("w1_raw", w1)
         unit_sb = keep.tile([P, PACK], F32, name="unit_sb")
         nc.sync.dma_start(unit_sb[:], unit.rearrange("(p t) o -> p (t o)", t=PACK))
@@ -67,12 +66,12 @@ def tile_picked_yvotepr_tru_p_kernel(tc, x_words, x_scales, w1, w2, unit, w3, of
 
         x_codes = keep.tile([P, S], U32, name="x_codes", align_bytes=64)
         x_bytes = keep.tile([P, S], U8, name="x_bytes", align_bytes=64)
-        nc.vector.tensor_copy(x_bytes[:], table_scales[:].indirect(offs_sb[:]))
         nc.vector.tensor_copy(x_codes[:], table_words[:].bitcast(U32).indirect(offs_sb[:]))
+        nc.vector.tensor_copy(x_bytes[:], table_scales[:].indirect(offs_sb[:]))
 
-        def round_pair(name, raw, pair):
+        def round_pair(copy, name, raw, pair):
             grouped = keep.tile([P, 2 * P * PACK], BF16, name=name, align_bytes=64)
-            nc.vector.tensor_copy(
+            copy(
                 grouped[:].rearrange("p (e m j) -> p m j e", e=2, j=PACK),
                 raw[:].rearrange("p j (m t) -> p m j t", t=PACK)[:, :, :, 2 * pair : 2 * pair + 2],
             )
@@ -101,57 +100,65 @@ def tile_picked_yvotepr_tru_p_kernel(tc, x_words, x_scales, w1, w2, unit, w3, of
             nc.scalar.activation(window[:], bank[:], COPY, scale=scale)
             return window
 
-        w1_bf = [round_pair("w1_bf%d" % e, w1_raw, e) for e in range(2)]
+        w1_bf = [round_pair(nc.vector.tensor_copy, "w1_bf0", w1_raw, 0), round_pair(nc.scalar.copy, "w1_bf1", w1_raw, 1)]
         w1_mx = [quantize(keep, "w1_%d" % e, w1_bf[e][:], 2 * P) for e in range(2)]
-        w2_bf = [round_pair("w2_bf%d" % e, w2_raw, e) for e in range(2)]
+        w2_bf = [round_pair(nc.vector.tensor_copy, "w2_bf%d" % e, w2_raw, e) for e in range(2)]
         w2_mx = [quantize(keep, "w2_%d" % e, w2_bf[e][:], 2 * P) for e in range(2)]
-        w3_bf = keep.tile([P, N * PACK], BF16, name="w3_bf", align_bytes=64)
-        nc.vector.tensor_copy(
-            w3_bf[:].rearrange("p (c e j) -> p c j e", e=2, j=PACK),
-            w3_raw[:].rearrange("p j (c e) -> p c j e", e=2),
-        )
-        w3_codes, w3_scales = quantize(keep, "w3", w3_bf[:], N)
 
         y_win, z_win = {}, {}
-        for c, (r0, n) in enumerate(CHUNKS):
+
+        def scalar_gathers(c):
+            r0, n = CHUNKS[c]
             cols = slice(r0 // LANES, (r0 + n) // LANES)
-            judged = items.tile([P, PACK, n], F32, name="judged")
+            a, b = {}, {}
             own = items.tile([P, PACK, n], F32, name="own")
             for pair in range(2):
                 ts = (2 * pair, 2 * pair + 1)
-                a, b, ab, abc = {}, {}, {}, {}
                 for t in ts:
                     if c == 0:
                         y_win[t] = project("y%d" % t, w1_mx, t, half_unit[:, t : t + 1])
                     a[t] = work.tile([P, n], F32, name="a")
                     nc.scalar.activation(a[t][:], y_win[t][:].indirect(va_sb[:, cols]), COPY)
-                    if (c, t) not in FUSED_VB:
+                    if c > 0:
                         b[t] = work.tile([P, n], F32, name="b")
                         nc.scalar.activation(b[t][:], y_win[t][:].indirect(vb_sb[:, cols]), COPY)
                 for t in ts:
                     if c == 0:
                         z_win[t] = project("z%d" % t, w2_mx, t, 2.0)
-                for t in ts:
-                    nc.scalar.activation(own[:, t, :], y_win[t][:].indirect(tr_sb[:, cols]), COPY)
-                for t in ts:
-                    ab[t] = work.tile([P, n], F32, name="ab")
-                    if (c, t) in FUSED_VB:
-                        nc.vector.tensor_tensor(ab[t][:], y_win[t][:].indirect(vb_sb[:, cols]), a[t][:], ADD)
-                    else:
-                        nc.vector.tensor_tensor(ab[t][:], b[t][:], a[t][:], ADD)
-                for t in ts:
-                    abc[t] = work.tile([P, n], F32, name="abc")
-                    nc.vector.tensor_tensor(abc[t][:], y_win[t][:].indirect(vc_sb[:, cols]), ab[t][:], ADD)
-                for t in ts:
-                    nc.vector.tensor_tensor(judged[:, t, :], z_win[t][:].indirect(tr_sb[:, cols]), abc[t][:], MULT)
+            for t in range(PACK):
+                nc.scalar.activation(own[:, t, :], y_win[t][:].indirect(tr_sb[:, cols]), COPY)
+            return a, b, own
 
-            hid = items.tile([P, n * PACK], BF16, name="hid", align_bytes=64)
+        def vector_steps(c, a, b, judged):
+            r0, n = CHUNKS[c]
+            cols = slice(r0 // LANES, (r0 + n) // LANES)
+            ab, abc = {}, {}
+
+            def add_b(t):
+                ab[t] = work.tile([P, n], F32, name="ab")
+                second = b[t][:] if c > 0 else y_win[t][:].indirect(vb_sb[:, cols])
+                nc.vector.tensor_tensor(ab[t][:], second, a[t][:], ADD)
+
+            def add_c(t):
+                abc[t] = work.tile([P, n], F32, name="abc")
+                nc.vector.tensor_tensor(abc[t][:], y_win[t][:].indirect(vc_sb[:, cols]), ab[t][:], ADD)
+
+            def judge(t):
+                nc.vector.tensor_tensor(judged[:, t, :], z_win[t][:].indirect(tr_sb[:, cols]), abc[t][:], MULT)
+
+            return [(step, t) for pair in range(2) for step in (add_b, add_c, judge) for t in (2 * pair, 2 * pair + 1)]
+
+        def round_hid(judged, own, part):
+            hid = items.tile([P, (part.stop - part.start) * PACK], BF16, name="hid", align_bytes=64)
             nc.vector.tensor_tensor(
                 hid[:].rearrange("p (c e t) -> p c t e", e=2, t=PACK),
-                judged[:].rearrange("p t (c e) -> p c t e", e=2),
-                own[:].rearrange("p t (c e) -> p c t e", e=2),
+                judged[:, :, part].rearrange("p t (c e) -> p c t e", e=2),
+                own[:, :, part].rearrange("p t (c e) -> p c t e", e=2),
                 ADD,
             )
+            return hid
+
+        def labels(hid, r0, n):
             hid_codes, hid_scales = quantize(items, "hid", hid[:], n)
             acc = last_psum.tile([P, n], F32, name="acc")
             for n0 in range(0, n, 256):
@@ -168,3 +175,27 @@ def tile_picked_yvotepr_tru_p_kernel(tc, x_words, x_scales, w1, w2, unit, w3, of
             result = items.tile([P, n], F32, name="result")
             nc.scalar.activation(result[:], acc[:], COPY)
             nc.sync.dma_start(out[:, r0 : r0 + n], result[:])
+
+        previous = None
+        for c, (r0, n) in enumerate(CHUNKS):
+            a, b, own = scalar_gathers(c)
+            judged = items.tile([P, PACK, n], F32, name="judged")
+            for i, (step, t) in enumerate(vector_steps(c, a, b, judged)):
+                step(t)
+                if c == 0 and i == 0:
+                    w3_bf = keep.tile([P, N * PACK], BF16, name="w3_bf", align_bytes=64)
+                    nc.vector.tensor_copy(
+                        w3_bf[:].rearrange("p (c e j) -> p c j e", e=2, j=PACK),
+                        w3_raw[:].rearrange("p j (c e) -> p c j e", e=2),
+                    )
+                if c == 0 and i == 1:
+                    w3_codes, w3_scales = quantize(keep, "w3", w3_bf[:], N)
+                if c > 0 and i == 1:
+                    hid = round_hid(previous[0], previous[1], slice(0, previous[3]))
+                if c > 0 and i == 2:
+                    labels(hid, previous[2], previous[3])
+            previous = (judged, own, r0, n)
+        judged, own, r0, n = previous
+        halves = [round_hid(judged, own, slice(h * n // 2, (h + 1) * n // 2)) for h in range(2)]
+        for h in range(2):
+            labels(halves[h], r0 + h * n // 2, n // 2)

@@ -19,6 +19,7 @@ P = 128
 PACK = 4
 LANES = 16
 CHUNKS = ((0, 384), (384, 384), (768, 256))
+FUSED_VB_TILES = 3
 
 
 def tile_picked_yvotepr_tru_p_kernel(tc, x_words, x_scales, w1, w2, unit, w3, offs, va, vb, vc, tr, out):
@@ -26,7 +27,7 @@ def tile_picked_yvotepr_tru_p_kernel(tc, x_words, x_scales, w1, w2, unit, w3, of
     with ExitStack() as ctx:
         lists = ctx.enter_context(tc.tile_pool(name="lists", bufs=1))
         keep = ctx.enter_context(tc.tile_pool(name="keep", bufs=1))
-        work = ctx.enter_context(tc.tile_pool(name="work", bufs=8))
+        work = ctx.enter_context(tc.tile_pool(name="work", bufs=12))
         items = ctx.enter_context(tc.tile_pool(name="items", bufs=3))
         first_psum = ctx.enter_context(tc.psum_pool(name="first_psum", bufs=4))
         last_psum = ctx.enter_context(tc.psum_pool(name="last_psum", bufs=4))
@@ -51,7 +52,7 @@ def tile_picked_yvotepr_tru_p_kernel(tc, x_words, x_scales, w1, w2, unit, w3, of
                 table_scales[32 * q : 32 * q + 4, :].bitcast(I32),
                 x_scales[0, 4 * q : 4 * q + 4, :].bitcast(I32),
             )
-        w1_raw = load_rows("w1_raw", w1)
+        w1_raw = [load_rows("w1_raw%d" % h, w1[:, h * H // 2 : (h + 1) * H // 2]) for h in range(2)]
         unit_sb = keep.tile([P, PACK], F32, name="unit_sb")
         nc.sync.dma_start(unit_sb[:], unit.rearrange("(p t) o -> p (t o)", t=PACK))
         va_sb = load_list("va_sb", va)
@@ -69,13 +70,12 @@ def tile_picked_yvotepr_tru_p_kernel(tc, x_words, x_scales, w1, w2, unit, w3, of
         nc.vector.tensor_copy(x_codes[:], table_words[:].bitcast(U32).indirect(offs_sb[:]))
         nc.vector.tensor_copy(x_bytes[:], table_scales[:].indirect(offs_sb[:]))
 
-        def round_pair(copy, name, raw, pair):
-            grouped = keep.tile([P, 2 * P * PACK], BF16, name=name, align_bytes=64)
+        def round_pair(copy, grouped, raw, pair, m0):
+            m = raw.shape[2] // PACK
             copy(
-                grouped[:].rearrange("p (e m j) -> p m j e", e=2, j=PACK),
+                grouped[:].rearrange("p (e m j) -> p m j e", e=2, j=PACK)[:, m0 : m0 + m],
                 raw[:].rearrange("p j (m t) -> p m j t", t=PACK)[:, :, :, 2 * pair : 2 * pair + 2],
             )
-            return grouped
 
         def quantize(pool, name, grouped, width):
             codes = pool.tile([P, width], U32, name=name + "_codes", align_bytes=64)
@@ -83,51 +83,73 @@ def tile_picked_yvotepr_tru_p_kernel(tc, x_words, x_scales, w1, w2, unit, w3, of
             nc.vector.quantize_mx(out=codes[:].bitcast(FP8X4), scales=scales[:], in_=grouped)
             return codes, scales
 
-        def project(name, weights, t, scale):
-            codes, scales = weights[t // 2]
-            cols = slice(P * (t % 2), P * (t % 2 + 1))
-            bank = first_psum.tile([P, S], F32, name="bank")
+        def product(weights, cols, picked):
+            codes, scales = weights
+            bank = first_psum.tile([P, picked.stop - picked.start], F32, name="bank")
             nc.tensor.matmul_mx(
                 out=bank[:],
                 lhsT=codes[:, cols].bitcast(FP8X4),
                 lhsT_scale=scales[:, cols],
-                rhs=x_codes[:].bitcast(FP8X4),
-                rhs_scale=x_bytes[:],
+                rhs=x_codes[:, picked].bitcast(FP8X4),
+                rhs_scale=x_bytes[:, picked],
                 start=True,
                 stop=True,
             )
+            return bank
+
+        def project(name, weights, cols, scale):
+            bank = product(weights, cols, slice(0, S))
             window = keep.tile([P, S], F32, name=name)
             nc.scalar.activation(window[:], bank[:], COPY, scale=scale)
             return window
 
-        w1_bf = [round_pair(nc.vector.tensor_copy, "w1_bf0", w1_raw, 0), round_pair(nc.scalar.copy, "w1_bf1", w1_raw, 1)]
-        w1_mx = [quantize(keep, "w1_%d" % e, w1_bf[e][:], 2 * P) for e in range(2)]
-        w2_bf = [round_pair(nc.vector.tensor_copy, "w2_bf%d" % e, w2_raw, e) for e in range(2)]
-        w2_mx = [quantize(keep, "w2_%d" % e, w2_bf[e][:], 2 * P) for e in range(2)]
+        w1_bf = [keep.tile([P, 2 * P * PACK], BF16, name="w1_bf%d" % e, align_bytes=64) for e in range(2)]
+        w2_bf = [keep.tile([P, 2 * P * PACK], BF16, name="w2_bf%d" % e, align_bytes=64) for e in range(2)]
+        round_pair(nc.scalar.copy, w1_bf[0], w1_raw[0], 0, 0)
+        round_pair(nc.scalar.copy, w1_bf[1], w1_raw[0], 1, 0)
+        round_pair(nc.vector.tensor_copy, w1_bf[0], w1_raw[1], 0, P // 2)
+        round_pair(nc.scalar.copy, w1_bf[1], w1_raw[1], 1, P // 2)
+        first, second = slice(0, P), slice(P, 2 * P)
+        w1_tile0 = quantize(keep, "w1_t0", w1_bf[0][:, : P * PACK], P)
+        w1_tile1 = quantize(keep, "w1_t1", w1_bf[0][:, P * PACK :], P)
+        w1_pair1 = quantize(keep, "w1_p1", w1_bf[1][:], 2 * P)
+        w1_mx = [(w1_tile0, first), (w1_tile1, first), (w1_pair1, first), (w1_pair1, second)]
 
         y_win, z_win = {}, {}
+        y_win[0] = keep.tile([P, S], F32, name="y0")
+        low, high = slice(0, S // 2), slice(S // 2, S)
+        nc.scalar.activation(y_win[0][:, low], product(w1_tile0, first, low)[:], COPY, scale=half_unit[:, 0:1])
+        nc.vector.tensor_scalar(y_win[0][:, high], product(w1_tile0, first, high)[:], half_unit[:, 0:1], None, MULT)
 
-        def scalar_gathers(c):
+        for e in range(2):
+            round_pair(nc.vector.tensor_copy, w2_bf[e], w2_raw, e, 0)
+        w2_pairs = [quantize(keep, "w2_p%d" % e, w2_bf[e][:], 2 * P) for e in range(2)]
+        w2_mx = [(w2_pairs[0], first), (w2_pairs[0], second), (w2_pairs[1], first), (w2_pairs[1], second)]
+
+        def fused_vb(c, t):
+            return c == 0 and t < FUSED_VB_TILES
+
+        def gather_own(c, own):
             r0, n = CHUNKS[c]
             cols = slice(r0 // LANES, (r0 + n) // LANES)
-            a, b = {}, {}
-            own = items.tile([P, PACK, n], F32, name="own")
-            for pair in range(2):
-                ts = (2 * pair, 2 * pair + 1)
-                for t in ts:
-                    if c == 0:
-                        y_win[t] = project("y%d" % t, w1_mx, t, half_unit[:, t : t + 1])
-                    a[t] = work.tile([P, n], F32, name="a")
-                    nc.scalar.activation(a[t][:], y_win[t][:].indirect(va_sb[:, cols]), COPY)
-                    if c > 0:
-                        b[t] = work.tile([P, n], F32, name="b")
-                        nc.scalar.activation(b[t][:], y_win[t][:].indirect(vb_sb[:, cols]), COPY)
-                for t in ts:
-                    if c == 0:
-                        z_win[t] = project("z%d" % t, w2_mx, t, 2.0)
             for t in range(PACK):
                 nc.scalar.activation(own[:, t, :], y_win[t][:].indirect(tr_sb[:, cols]), COPY)
-            return a, b, own
+
+        def scalar_gathers(c, pair, a, b):
+            r0, n = CHUNKS[c]
+            cols = slice(r0 // LANES, (r0 + n) // LANES)
+            ts = (2 * pair, 2 * pair + 1)
+            for t in ts:
+                if t not in y_win:
+                    y_win[t] = project("y%d" % t, *w1_mx[t], half_unit[:, t : t + 1])
+                a[t] = work.tile([P, n], F32, name="a")
+                nc.scalar.activation(a[t][:], y_win[t][:].indirect(va_sb[:, cols]), COPY)
+                if not fused_vb(c, t):
+                    b[t] = work.tile([P, n], F32, name="b")
+                    nc.scalar.activation(b[t][:], y_win[t][:].indirect(vb_sb[:, cols]), COPY)
+            for t in ts:
+                if t not in z_win:
+                    z_win[t] = project("z%d" % t, *w2_mx[t], 2.0)
 
         def vector_steps(c, a, b, judged):
             r0, n = CHUNKS[c]
@@ -136,8 +158,8 @@ def tile_picked_yvotepr_tru_p_kernel(tc, x_words, x_scales, w1, w2, unit, w3, of
 
             def add_b(t):
                 ab[t] = work.tile([P, n], F32, name="ab")
-                second = b[t][:] if c > 0 else y_win[t][:].indirect(vb_sb[:, cols])
-                nc.vector.tensor_tensor(ab[t][:], second, a[t][:], ADD)
+                vb_vote = y_win[t][:].indirect(vb_sb[:, cols]) if fused_vb(c, t) else b[t][:]
+                nc.vector.tensor_tensor(ab[t][:], vb_vote, a[t][:], ADD)
 
             def add_c(t):
                 abc[t] = work.tile([P, n], F32, name="abc")
@@ -178,21 +200,28 @@ def tile_picked_yvotepr_tru_p_kernel(tc, x_words, x_scales, w1, w2, unit, w3, of
 
         previous = None
         for c, (r0, n) in enumerate(CHUNKS):
-            a, b, own = scalar_gathers(c)
+            a, b = {}, {}
+            own = items.tile([P, PACK, n], F32, name="own")
+            scalar_gathers(c, 0, a, b)
+            if c > 0:
+                gather_own(c - 1, previous[1])
+            scalar_gathers(c, 1, a, b)
+            if c == len(CHUNKS) - 1:
+                gather_own(c, own)
             judged = items.tile([P, PACK, n], F32, name="judged")
             for i, (step, t) in enumerate(vector_steps(c, a, b, judged)):
                 step(t)
-                if c == 0 and i == 0:
+                if c == 0 and i == 6:
                     w3_bf = keep.tile([P, N * PACK], BF16, name="w3_bf", align_bytes=64)
                     nc.vector.tensor_copy(
                         w3_bf[:].rearrange("p (c e j) -> p c j e", e=2, j=PACK),
                         w3_raw[:].rearrange("p j (c e) -> p c j e", e=2),
                     )
-                if c == 0 and i == 1:
+                if c == 0 and i == 7:
                     w3_codes, w3_scales = quantize(keep, "w3", w3_bf[:], N)
-                if c > 0 and i == 1:
+                if c > 0 and i == 5:
                     hid = round_hid(previous[0], previous[1], slice(0, previous[3]))
-                if c > 0 and i == 2:
+                if c > 0 and i == 6:
                     labels(hid, previous[2], previous[3])
             previous = (judged, own, r0, n)
         judged, own, r0, n = previous

@@ -18,8 +18,11 @@ COPY = mybir.ActivationFunctionType.Copy
 P = 128
 PACK = 4
 LANES = 16
-CHUNKS = ((0, 384), (384, 384), (768, 256))
-FUSED_VB_TILES = 3
+WINDOW = U + 16
+PARTS = ((0, 512), (512, 256), (768, 128), (896, 128))
+HALVES = (slice(0, U // 2), slice(U // 2, U))
+OWN_PARTS = (slice(0, 512), slice(512, 768), slice(768, 1024))
+FUSED_VB_TILES = 2
 
 
 def tile_picked_yvotepr_tru_p_kernel(tc, x_words, x_scales, w1, w2, unit, w3, offs, va, vb, vc, tr, out):
@@ -27,8 +30,8 @@ def tile_picked_yvotepr_tru_p_kernel(tc, x_words, x_scales, w1, w2, unit, w3, of
     with ExitStack() as ctx:
         lists = ctx.enter_context(tc.tile_pool(name="lists", bufs=1))
         keep = ctx.enter_context(tc.tile_pool(name="keep", bufs=1))
-        work = ctx.enter_context(tc.tile_pool(name="work", bufs=12))
-        items = ctx.enter_context(tc.tile_pool(name="items", bufs=3))
+        work = ctx.enter_context(tc.tile_pool(name="work", bufs=4))
+        items = ctx.enter_context(tc.tile_pool(name="items", bufs=4))
         first_psum = ctx.enter_context(tc.psum_pool(name="first_psum", bufs=4))
         last_psum = ctx.enter_context(tc.psum_pool(name="last_psum", bufs=4))
 
@@ -44,6 +47,10 @@ def tile_picked_yvotepr_tru_p_kernel(tc, x_words, x_scales, w1, w2, unit, w3, of
 
         table_scales = keep.tile([P, T], U8, name="table_scales")
         nc.gpsimd.memset(table_scales[:].bitcast(I32), 0)
+        y_win = [keep.tile([P, WINDOW], F32, name="y%d" % t) for t in range(PACK)]
+        z_win = [keep.tile([P, WINDOW], F32, name="z%d" % t) for t in range(PACK)]
+        for window in y_win + z_win:
+            nc.gpsimd.memset(window[:, S:], 0.0)
         offs_sb = load_list("offs_sb", offs)
         table_words = keep.tile([P, T], I32, name="table_words")
         nc.sync.dma_start(table_words[:], x_words[0].rearrange("p n r -> p (n r)").bitcast(I32))
@@ -97,11 +104,8 @@ def tile_picked_yvotepr_tru_p_kernel(tc, x_words, x_scales, w1, w2, unit, w3, of
             )
             return bank
 
-        def project(name, weights, cols, scale):
-            bank = product(weights, cols, slice(0, S))
-            window = keep.tile([P, S], F32, name=name)
-            nc.scalar.activation(window[:], bank[:], COPY, scale=scale)
-            return window
+        def project(window, weights, cols, scale):
+            nc.scalar.activation(window[:, :S], product(weights, cols, slice(0, S))[:], COPY, scale=scale)
 
         w1_bf = [keep.tile([P, 2 * P * PACK], BF16, name="w1_bf%d" % e, align_bytes=64) for e in range(2)]
         w2_bf = [keep.tile([P, 2 * P * PACK], BF16, name="w2_bf%d" % e, align_bytes=64) for e in range(2)]
@@ -115,8 +119,6 @@ def tile_picked_yvotepr_tru_p_kernel(tc, x_words, x_scales, w1, w2, unit, w3, of
         w1_pair1 = quantize(keep, "w1_p1", w1_bf[1][:], 2 * P)
         w1_mx = [(w1_tile0, first), (w1_tile1, first), (w1_pair1, first), (w1_pair1, second)]
 
-        y_win, z_win = {}, {}
-        y_win[0] = keep.tile([P, S], F32, name="y0")
         low, high = slice(0, S // 2), slice(S // 2, S)
         nc.scalar.activation(y_win[0][:, low], product(w1_tile0, first, low)[:], COPY, scale=half_unit[:, 0:1])
         nc.vector.tensor_scalar(y_win[0][:, high], product(w1_tile0, first, high)[:], half_unit[:, 0:1], None, MULT)
@@ -126,56 +128,65 @@ def tile_picked_yvotepr_tru_p_kernel(tc, x_words, x_scales, w1, w2, unit, w3, of
         w2_pairs = [quantize(keep, "w2_p%d" % e, w2_bf[e][:], 2 * P) for e in range(2)]
         w2_mx = [(w2_pairs[0], first), (w2_pairs[0], second), (w2_pairs[1], first), (w2_pairs[1], second)]
 
-        def fused_vb(c, t):
-            return c == 0 and t < FUSED_VB_TILES
+        def entries(offsets, part):
+            return offsets[:, part.start // LANES : part.stop // LANES]
 
-        def gather_own(c, own):
-            r0, n = CHUNKS[c]
-            cols = slice(r0 // LANES, (r0 + n) // LANES)
+        a, b = {}, {}
+        for t in range(PACK):
+            if t > 0:
+                project(y_win[t], *w1_mx[t], half_unit[:, t : t + 1])
+            a[t] = work.tile([P, U], F32, name="a")
+            nc.scalar.activation(a[t][:], y_win[t][:].indirect(va_sb[:]), COPY)
+            if t >= FUSED_VB_TILES:
+                b[t] = work.tile([P, U], F32, name="b")
+                nc.scalar.activation(b[t][:], y_win[t][:].indirect(vb_sb[:]), COPY)
+            if t > 0:
+                project(z_win[t - 1], *w2_mx[t - 1], 2.0)
+        project(z_win[PACK - 1], *w2_mx[PACK - 1], 2.0)
+        own = {}
+        for part in OWN_PARTS:
+            own[part.start] = keep.tile([P, PACK, part.stop - part.start], F32, name="own%d" % part.start)
             for t in range(PACK):
-                nc.scalar.activation(own[:, t, :], y_win[t][:].indirect(tr_sb[:, cols]), COPY)
+                nc.scalar.activation(own[part.start][:, t, :], y_win[t][:].indirect(entries(tr_sb, part)), COPY)
 
-        def scalar_gathers(c, pair, a, b):
-            r0, n = CHUNKS[c]
-            cols = slice(r0 // LANES, (r0 + n) // LANES)
-            ts = (2 * pair, 2 * pair + 1)
-            for t in ts:
-                if t not in y_win:
-                    y_win[t] = project("y%d" % t, *w1_mx[t], half_unit[:, t : t + 1])
-                a[t] = work.tile([P, n], F32, name="a")
-                nc.scalar.activation(a[t][:], y_win[t][:].indirect(va_sb[:, cols]), COPY)
-                if not fused_vb(c, t):
-                    b[t] = work.tile([P, n], F32, name="b")
-                    nc.scalar.activation(b[t][:], y_win[t][:].indirect(vb_sb[:, cols]), COPY)
-            for t in ts:
-                if t not in z_win:
-                    z_win[t] = project("z%d" % t, *w2_mx[t], 2.0)
+        ab = [work.tile([P, U], F32, name="ab") for t in range(PACK)]
+        abc = [work.tile([P, U], F32, name="abc") for t in range(PACK)]
+        judged = keep.tile([P, PACK, U], F32, name="judged")
+        whole = slice(0, U)
 
-        def vector_steps(c, a, b, judged):
-            r0, n = CHUNKS[c]
-            cols = slice(r0 // LANES, (r0 + n) // LANES)
-            ab, abc = {}, {}
+        def add_b(t):
+            vb_vote = b[t][:] if t >= FUSED_VB_TILES else y_win[t][:].indirect(vb_sb[:])
+            nc.vector.tensor_tensor(ab[t][:], vb_vote, a[t][:], ADD)
 
-            def add_b(t):
-                ab[t] = work.tile([P, n], F32, name="ab")
-                vb_vote = y_win[t][:].indirect(vb_sb[:, cols]) if fused_vb(c, t) else b[t][:]
-                nc.vector.tensor_tensor(ab[t][:], vb_vote, a[t][:], ADD)
+        def add_c(t, part):
+            nc.vector.tensor_tensor(abc[t][:, part], y_win[t][:].indirect(entries(vc_sb, part)), ab[t][:, part], ADD)
 
-            def add_c(t):
-                abc[t] = work.tile([P, n], F32, name="abc")
-                nc.vector.tensor_tensor(abc[t][:], y_win[t][:].indirect(vc_sb[:, cols]), ab[t][:], ADD)
+        def judge(t, part):
+            nc.vector.tensor_tensor(judged[:, t, part], z_win[t][:].indirect(entries(tr_sb, part)), abc[t][:, part], MULT)
 
-            def judge(t):
-                nc.vector.tensor_tensor(judged[:, t, :], z_win[t][:].indirect(tr_sb[:, cols]), abc[t][:], MULT)
+        add_b(0)
+        w3_bf = keep.tile([P, N * PACK], BF16, name="w3_bf", align_bytes=64)
+        nc.vector.tensor_copy(
+            w3_bf[:].rearrange("p (c e j) -> p c j e", e=2, j=PACK),
+            w3_raw[:].rearrange("p j (c e) -> p c j e", e=2),
+        )
+        for t in range(PACK - 1):
+            add_c(t, whole)
+            add_b(t + 1)
+            if t == 0:
+                w3_codes, w3_scales = quantize(keep, "w3", w3_bf[:], N)
+            judge(t, whole)
+        for step in (add_c, judge):
+            for part in HALVES:
+                step(PACK - 1, part)
 
-            return [(step, t) for pair in range(2) for step in (add_b, add_c, judge) for t in (2 * pair, 2 * pair + 1)]
-
-        def round_hid(judged, own, part):
-            hid = items.tile([P, (part.stop - part.start) * PACK], BF16, name="hid", align_bytes=64)
+        def round_hid(r0, n):
+            own0 = max(start for start in own if start <= r0)
+            hid = items.tile([P, n * PACK], BF16, name="hid", align_bytes=64)
             nc.vector.tensor_tensor(
                 hid[:].rearrange("p (c e t) -> p c t e", e=2, t=PACK),
-                judged[:, :, part].rearrange("p t (c e) -> p c t e", e=2),
-                own[:, :, part].rearrange("p t (c e) -> p c t e", e=2),
+                judged[:, :, r0 : r0 + n].rearrange("p t (c e) -> p c t e", e=2),
+                own[own0][:, :, r0 - own0 : r0 - own0 + n].rearrange("p t (c e) -> p c t e", e=2),
                 ADD,
             )
             return hid
@@ -183,48 +194,21 @@ def tile_picked_yvotepr_tru_p_kernel(tc, x_words, x_scales, w1, w2, unit, w3, of
         def labels(hid, r0, n):
             hid_codes, hid_scales = quantize(items, "hid", hid[:], n)
             acc = last_psum.tile([P, n], F32, name="acc")
-            for n0 in range(0, n, 256):
-                part = slice(n0, min(n0 + 256, n))
-                nc.tensor.matmul_mx(
-                    out=acc[:, part],
-                    lhsT=w3_codes[:].bitcast(FP8X4),
-                    lhsT_scale=w3_scales[:],
-                    rhs=hid_codes[:, part].bitcast(FP8X4),
-                    rhs_scale=hid_scales[:, part],
-                    start=True,
-                    stop=True,
-                )
+            nc.tensor.matmul_mx(
+                out=acc[:],
+                lhsT=w3_codes[:].bitcast(FP8X4),
+                lhsT_scale=w3_scales[:],
+                rhs=hid_codes[:].bitcast(FP8X4),
+                rhs_scale=hid_scales[:],
+                start=True,
+                stop=True,
+            )
             result = items.tile([P, n], F32, name="result")
             nc.scalar.activation(result[:], acc[:], COPY)
             nc.sync.dma_start(out[:, r0 : r0 + n], result[:])
 
-        previous = None
-        for c, (r0, n) in enumerate(CHUNKS):
-            a, b = {}, {}
-            own = items.tile([P, PACK, n], F32, name="own")
-            scalar_gathers(c, 0, a, b)
-            if c > 0:
-                gather_own(c - 1, previous[1])
-            scalar_gathers(c, 1, a, b)
-            if c == len(CHUNKS) - 1:
-                gather_own(c, own)
-            judged = items.tile([P, PACK, n], F32, name="judged")
-            for i, (step, t) in enumerate(vector_steps(c, a, b, judged)):
-                step(t)
-                if c == 0 and i == 6:
-                    w3_bf = keep.tile([P, N * PACK], BF16, name="w3_bf", align_bytes=64)
-                    nc.vector.tensor_copy(
-                        w3_bf[:].rearrange("p (c e j) -> p c j e", e=2, j=PACK),
-                        w3_raw[:].rearrange("p j (c e) -> p c j e", e=2),
-                    )
-                if c == 0 and i == 7:
-                    w3_codes, w3_scales = quantize(keep, "w3", w3_bf[:], N)
-                if c > 0 and i == 5:
-                    hid = round_hid(previous[0], previous[1], slice(0, previous[3]))
-                if c > 0 and i == 6:
-                    labels(hid, previous[2], previous[3])
-            previous = (judged, own, r0, n)
-        judged, own, r0, n = previous
-        halves = [round_hid(judged, own, slice(h * n // 2, (h + 1) * n // 2)) for h in range(2)]
-        for h in range(2):
-            labels(halves[h], r0 + h * n // 2, n // 2)
+        hid = round_hid(*PARTS[0])
+        for i, part in enumerate(PARTS):
+            ahead = round_hid(*PARTS[i + 1]) if i + 1 < len(PARTS) else None
+            labels(hid, *part)
+            hid = ahead

@@ -18,11 +18,15 @@ COPY = mybir.ActivationFunctionType.Copy
 P = 128
 PACK = 4
 LANES = 16
-WINDOW = U + 16
-PARTS = ((0, 512), (512, 256), (768, 128), (896, 128))
+QUADRANT = 32
+
+WINDOW = U + LANES
+
+ALL_ITEMS = slice(0, U)
 HALVES = (slice(0, U // 2), slice(U // 2, U))
-OWN_PARTS = (slice(0, 512), slice(512, 768), slice(768, 1024))
-FUSED_VB_TILES = 2
+OPENING = (slice(0, U // 4), slice(U // 4, U))
+OWN_PIECES = (slice(0, U // 2), slice(U // 2, 3 * U // 4), slice(3 * U // 4, U))
+LABEL_PIECES = OWN_PIECES[:2] + (slice(3 * U // 4, 7 * U // 8), slice(7 * U // 8, U))
 
 
 def tile_picked_yvotepr_tru_p_kernel(tc, x_words, x_scales, w1, w2, unit, w3, offs, va, vb, vc, tr, out):
@@ -30,10 +34,12 @@ def tile_picked_yvotepr_tru_p_kernel(tc, x_words, x_scales, w1, w2, unit, w3, of
     with ExitStack() as ctx:
         lists = ctx.enter_context(tc.tile_pool(name="lists", bufs=1))
         keep = ctx.enter_context(tc.tile_pool(name="keep", bufs=1))
-        work = ctx.enter_context(tc.tile_pool(name="work", bufs=4))
-        items = ctx.enter_context(tc.tile_pool(name="items", bufs=4))
-        first_psum = ctx.enter_context(tc.psum_pool(name="first_psum", bufs=4))
-        last_psum = ctx.enter_context(tc.psum_pool(name="last_psum", bufs=4))
+        pieces = ctx.enter_context(tc.tile_pool(name="pieces", bufs=len(LABEL_PIECES)))
+        first_psum = ctx.enter_context(tc.psum_pool(name="first_psum", bufs=PACK))
+        last_psum = ctx.enter_context(tc.psum_pool(name="last_psum", bufs=len(LABEL_PIECES)))
+
+        def row_tiles(name, width):
+            return [keep.tile([P, width], F32, name="%s%d" % (name, t)) for t in range(PACK)]
 
         def load_list(name, src):
             tile = lists.tile([P, src.shape[1]], U16, name=name)
@@ -45,23 +51,30 @@ def tile_picked_yvotepr_tru_p_kernel(tc, x_words, x_scales, w1, w2, unit, w3, of
             nc.sync.dma_start(raw[:], w.rearrange("(p j) c -> p j c", j=PACK))
             return raw
 
+        def width(items):
+            return items.stop - items.start
+
+        def entries(offsets, items):
+            return offsets[:, items.start // LANES : items.stop // LANES]
+
         table_scales = keep.tile([P, T], U8, name="table_scales")
         nc.gpsimd.memset(table_scales[:].bitcast(I32), 0)
-        y_win = [keep.tile([P, WINDOW], F32, name="y%d" % t) for t in range(PACK)]
-        z_win = [keep.tile([P, WINDOW], F32, name="z%d" % t) for t in range(PACK)]
-        for window in y_win + z_win:
-            nc.gpsimd.memset(window[:, S:], 0.0)
+        unit_sb = keep.tile([P, PACK], F32, name="unit_sb")
+        nc.gpsimd.dma_start(unit_sb[:], unit.rearrange("(p t) o -> p (t o)", t=PACK))
+        y_win, z_win = row_tiles("y_win", WINDOW), row_tiles("z_win", WINDOW)
+        for t in range(PACK):
+            nc.vector.memset(y_win[t][:, S:], 0.0)
+            nc.gpsimd.memset(z_win[t][:, S:], 0.0)
+
         offs_sb = load_list("offs_sb", offs)
         table_words = keep.tile([P, T], I32, name="table_words")
-        nc.sync.dma_start(table_words[:], x_words[0].rearrange("p n r -> p (n r)").bitcast(I32))
-        for q in range(4):
+        nc.sync.dma_start(table_words[:], x_words[0].rearrange("p n j -> p (n j)").bitcast(I32))
+        for q in range(P // QUADRANT):
             nc.sync.dma_start(
-                table_scales[32 * q : 32 * q + 4, :].bitcast(I32),
-                x_scales[0, 4 * q : 4 * q + 4, :].bitcast(I32),
+                table_scales[QUADRANT * q : QUADRANT * q + PACK, :].bitcast(I32),
+                x_scales[0, PACK * q : PACK * (q + 1), :].bitcast(I32),
             )
-        w1_raw = [load_rows("w1_raw%d" % h, w1[:, h * H // 2 : (h + 1) * H // 2]) for h in range(2)]
-        unit_sb = keep.tile([P, PACK], F32, name="unit_sb")
-        nc.sync.dma_start(unit_sb[:], unit.rearrange("(p t) o -> p (t o)", t=PACK))
+        w1_left, w1_right = load_rows("w1_left", w1[:, : H // 2]), load_rows("w1_right", w1[:, H // 2 :])
         va_sb = load_list("va_sb", va)
         w2_raw = load_rows("w2_raw", w2)
         vb_sb = load_list("vb_sb", vb)
@@ -69,146 +82,141 @@ def tile_picked_yvotepr_tru_p_kernel(tc, x_words, x_scales, w1, w2, unit, w3, of
         tr_sb = load_list("tr_sb", tr)
         w3_raw = load_rows("w3_raw", w3)
 
-        half_unit = keep.tile([P, PACK], F32, name="half_unit")
-        nc.scalar.activation(half_unit[:], unit_sb[:], COPY, scale=0.5)
-
         x_codes = keep.tile([P, S], U32, name="x_codes", align_bytes=64)
         x_bytes = keep.tile([P, S], U8, name="x_bytes", align_bytes=64)
         nc.vector.tensor_copy(x_codes[:], table_words[:].bitcast(U32).indirect(offs_sb[:]))
         nc.vector.tensor_copy(x_bytes[:], table_scales[:].indirect(offs_sb[:]))
 
-        def round_pair(copy, grouped, raw, pair, m0):
-            m = raw.shape[2] // PACK
+        def round_pair(copy, rounded, raw, pair, m0):
             copy(
-                grouped[:].rearrange("p (e m j) -> p m j e", e=2, j=PACK)[:, m0 : m0 + m],
+                rounded[:].rearrange("p (e m j) -> p m j e", e=2, j=PACK)[:, m0 : m0 + raw.shape[2] // PACK],
                 raw[:].rearrange("p j (m t) -> p m j t", t=PACK)[:, :, :, 2 * pair : 2 * pair + 2],
             )
 
-        def quantize(pool, name, grouped, width):
-            codes = pool.tile([P, width], U32, name=name + "_codes", align_bytes=64)
-            scales = pool.tile([P, width], U8, name=name + "_scales", align_bytes=64)
-            nc.vector.quantize_mx(out=codes[:].bitcast(FP8X4), scales=scales[:], in_=grouped)
+        def quantize(pool, name, rounded, words):
+            codes = pool.tile([P, words], U32, name=name + "_codes", align_bytes=64)
+            scales = pool.tile([P, words], U8, name=name + "_scales", align_bytes=64)
+            nc.vector.quantize_mx(out=codes[:].bitcast(FP8X4), scales=scales[:], in_=rounded)
             return codes, scales
 
-        def product(weights, cols, picked):
-            codes, scales = weights
-            bank = first_psum.tile([P, picked.stop - picked.start], F32, name="bank")
+        def multiply(pool, stationary, cols, moving, moving_cols):
+            bank = pool.tile([P, width(moving_cols)], F32, name="bank")
             nc.tensor.matmul_mx(
                 out=bank[:],
-                lhsT=codes[:, cols].bitcast(FP8X4),
-                lhsT_scale=scales[:, cols],
-                rhs=x_codes[:, picked].bitcast(FP8X4),
-                rhs_scale=x_bytes[:, picked],
+                lhsT=stationary[0][:, cols].bitcast(FP8X4),
+                lhsT_scale=stationary[1][:, cols],
+                rhs=moving[0][:, moving_cols].bitcast(FP8X4),
+                rhs_scale=moving[1][:, moving_cols],
                 start=True,
                 stop=True,
             )
             return bank
 
-        def project(window, weights, cols, scale):
-            nc.scalar.activation(window[:, :S], product(weights, cols, slice(0, S))[:], COPY, scale=scale)
+        def project(stationary, cols, picked):
+            return multiply(first_psum, stationary, cols, (x_codes, x_bytes), picked)
 
-        w1_bf = [keep.tile([P, 2 * P * PACK], BF16, name="w1_bf%d" % e, align_bytes=64) for e in range(2)]
-        w2_bf = [keep.tile([P, 2 * P * PACK], BF16, name="w2_bf%d" % e, align_bytes=64) for e in range(2)]
-        round_pair(nc.scalar.copy, w1_bf[0], w1_raw[0], 0, 0)
-        round_pair(nc.scalar.copy, w1_bf[1], w1_raw[0], 1, 0)
-        round_pair(nc.vector.tensor_copy, w1_bf[0], w1_raw[1], 0, P // 2)
-        round_pair(nc.scalar.copy, w1_bf[1], w1_raw[1], 1, P // 2)
         first, second = slice(0, P), slice(P, 2 * P)
-        w1_tile0 = quantize(keep, "w1_t0", w1_bf[0][:, : P * PACK], P)
-        w1_tile1 = quantize(keep, "w1_t1", w1_bf[0][:, P * PACK :], P)
-        w1_pair1 = quantize(keep, "w1_p1", w1_bf[1][:], 2 * P)
+        w1_bf = [keep.tile([P, 2 * P * PACK], BF16, name="w1_bf%d" % pair, align_bytes=64) for pair in range(2)]
+        w2_bf = [keep.tile([P, 2 * P * PACK], BF16, name="w2_bf%d" % pair, align_bytes=64) for pair in range(2)]
+
+        round_pair(nc.scalar.copy, w1_bf[0], w1_left, 0, 0)
+        round_pair(nc.scalar.copy, w1_bf[1], w1_left, 1, 0)
+        round_pair(nc.vector.tensor_copy, w1_bf[0], w1_right, 0, P // 2)
+        round_pair(nc.scalar.copy, w1_bf[1], w1_right, 1, P // 2)
+        w1_tile0 = quantize(keep, "w1_tile0", w1_bf[0][:, : P * PACK], P)
+        w1_tile1 = quantize(keep, "w1_tile1", w1_bf[0][:, P * PACK :], P)
+        w1_pair1 = quantize(keep, "w1_pair1", w1_bf[1][:], 2 * P)
         w1_mx = [(w1_tile0, first), (w1_tile1, first), (w1_pair1, first), (w1_pair1, second)]
 
         low, high = slice(0, S // 2), slice(S // 2, S)
-        nc.scalar.activation(y_win[0][:, low], product(w1_tile0, first, low)[:], COPY, scale=half_unit[:, 0:1])
-        nc.vector.tensor_scalar(y_win[0][:, high], product(w1_tile0, first, high)[:], half_unit[:, 0:1], None, MULT)
+        nc.scalar.activation(y_win[0][:, low], project(*w1_mx[0], low)[:], COPY, scale=unit_sb[:, 0:1])
+        nc.vector.tensor_scalar(y_win[0][:, high], project(*w1_mx[0], high)[:], unit_sb[:, 0:1], None, MULT)
 
-        for e in range(2):
-            round_pair(nc.vector.tensor_copy, w2_bf[e], w2_raw, e, 0)
-        w2_pairs = [quantize(keep, "w2_p%d" % e, w2_bf[e][:], 2 * P) for e in range(2)]
-        w2_mx = [(w2_pairs[0], first), (w2_pairs[0], second), (w2_pairs[1], first), (w2_pairs[1], second)]
+        for pair in range(2):
+            round_pair(nc.vector.tensor_copy, w2_bf[pair], w2_raw, pair, 0)
+        w2_pairs = [quantize(keep, "w2_pair%d" % pair, w2_bf[pair][:], 2 * P) for pair in range(2)]
+        w2_mx = [(w2_pairs[t // 2], (first, second)[t % 2]) for t in range(PACK)]
 
-        def entries(offsets, part):
-            return offsets[:, part.start // LANES : part.stop // LANES]
-
-        a, b = {}, {}
-        for t in range(PACK):
-            if t > 0:
-                project(y_win[t], *w1_mx[t], half_unit[:, t : t + 1])
-            a[t] = work.tile([P, U], F32, name="a")
-            nc.scalar.activation(a[t][:], y_win[t][:].indirect(va_sb[:]), COPY)
-            if t >= FUSED_VB_TILES:
-                b[t] = work.tile([P, U], F32, name="b")
-                nc.scalar.activation(b[t][:], y_win[t][:].indirect(vb_sb[:]), COPY)
-            if t > 0:
-                project(z_win[t - 1], *w2_mx[t - 1], 2.0)
-        project(z_win[PACK - 1], *w2_mx[PACK - 1], 2.0)
-        own = {}
-        for part in OWN_PARTS:
-            own[part.start] = keep.tile([P, PACK, part.stop - part.start], F32, name="own%d" % part.start)
-            for t in range(PACK):
-                nc.scalar.activation(own[part.start][:, t, :], y_win[t][:].indirect(entries(tr_sb, part)), COPY)
-
-        ab = [work.tile([P, U], F32, name="ab") for t in range(PACK)]
-        abc = [work.tile([P, U], F32, name="abc") for t in range(PACK)]
+        vote_a, vote_ab, vote_abc = row_tiles("vote_a", U), row_tiles("vote_ab", U), row_tiles("vote_abc", U)
         judged = keep.tile([P, PACK, U], F32, name="judged")
-        whole = slice(0, U)
 
-        def add_b(t):
-            vb_vote = b[t][:] if t >= FUSED_VB_TILES else y_win[t][:].indirect(vb_sb[:])
-            nc.vector.tensor_tensor(ab[t][:], vb_vote, a[t][:], ADD)
+        def fill(window, weights, scale):
+            nc.scalar.activation(window[:, :S], project(*weights, slice(0, S))[:], COPY, scale=scale)
 
-        def add_c(t, part):
-            nc.vector.tensor_tensor(abc[t][:, part], y_win[t][:].indirect(entries(vc_sb, part)), ab[t][:, part], ADD)
+        def gather(dst, t, offsets, items, scale=1.0):
+            nc.scalar.activation(dst, y_win[t][:].indirect(entries(offsets, items)), COPY, scale=scale)
 
-        def judge(t, part):
-            nc.vector.tensor_tensor(judged[:, t, part], z_win[t][:].indirect(entries(tr_sb, part)), abc[t][:, part], MULT)
+        def add_b_fused(t, items):
+            nc.vector.tensor_tensor(
+                vote_ab[t][:, items], y_win[t][:].indirect(entries(vb_sb, items)), vote_a[t][:, items], ADD
+            )
 
-        add_b(0)
+        def add_c(t, items):
+            nc.vector.tensor_tensor(
+                vote_abc[t][:, items], y_win[t][:].indirect(entries(vc_sb, items)), vote_ab[t][:, items], ADD
+            )
+
+        def judge(t, items):
+            nc.vector.tensor_tensor(
+                judged[:, t, items], z_win[t][:].indirect(entries(tr_sb, items)), vote_abc[t][:, items], MULT
+            )
+
+        for items in OPENING:
+            gather(vote_a[0][:, items], 0, va_sb, items)
+            add_b_fused(0, items)
+
         w3_bf = keep.tile([P, N * PACK], BF16, name="w3_bf", align_bytes=64)
         nc.vector.tensor_copy(
             w3_bf[:].rearrange("p (c e j) -> p c j e", e=2, j=PACK),
             w3_raw[:].rearrange("p j (c e) -> p c j e", e=2),
         )
-        for t in range(PACK - 1):
-            add_c(t, whole)
-            add_b(t + 1)
-            if t == 0:
-                w3_codes, w3_scales = quantize(keep, "w3", w3_bf[:], N)
-            judge(t, whole)
-        for step in (add_c, judge):
-            for part in HALVES:
-                step(PACK - 1, part)
 
-        def round_hid(r0, n):
-            own0 = max(start for start in own if start <= r0)
-            hid = items.tile([P, n * PACK], BF16, name="hid", align_bytes=64)
+        for t in range(1, PACK):
+            fill(y_win[t], w1_mx[t], unit_sb[:, t : t + 1])
+            gather(vote_a[t][:], t, va_sb, ALL_ITEMS)
+            vote_b = keep.tile([P, U], F32, name="vote_b%d" % t)
+            gather(vote_b[:], t, vb_sb, ALL_ITEMS)
+            fill(z_win[t - 1], w2_mx[t - 1], 1.0)
+            add_c(t - 1, ALL_ITEMS)
+            nc.vector.tensor_tensor(vote_ab[t][:], vote_b[:], vote_a[t][:], ADD)
+            judge(t - 1, ALL_ITEMS)
+        last = PACK - 1
+        w3_mx = quantize(keep, "w3", w3_bf[:], N)
+
+        vote_c = keep.tile([P, width(HALVES[1])], F32, name="vote_c")
+        gather(vote_c[:], last, vc_sb, HALVES[1])
+        fill(z_win[last], w2_mx[last], 1.0)
+        add_c(last, HALVES[0])
+        nc.vector.tensor_tensor(vote_abc[last][:, HALVES[1]], vote_c[:], vote_ab[last][:, HALVES[1]], ADD)
+        for items in HALVES:
+            judge(last, items)
+
+        own = {}
+        for items in OWN_PIECES:
+            own[items.start] = keep.tile([P, PACK, width(items)], F32, name="own%d" % items.start)
+            for t in range(PACK):
+                gather(own[items.start][:, t, :], t, tr_sb, items, scale=0.5)
+
+        def round_hid(items):
+            own_start = max(start for start in own if start <= items.start)
+            hid = pieces.tile([P, width(items) * PACK], BF16, name="hid", align_bytes=64)
             nc.vector.tensor_tensor(
                 hid[:].rearrange("p (c e t) -> p c t e", e=2, t=PACK),
-                judged[:, :, r0 : r0 + n].rearrange("p t (c e) -> p c t e", e=2),
-                own[own0][:, :, r0 - own0 : r0 - own0 + n].rearrange("p t (c e) -> p c t e", e=2),
+                judged[:, :, items].rearrange("p t (c e) -> p c t e", e=2),
+                own[own_start][:, :, items.start - own_start : items.stop - own_start].rearrange(
+                    "p t (c e) -> p c t e", e=2
+                ),
                 ADD,
             )
             return hid
 
-        def labels(hid, r0, n):
-            hid_codes, hid_scales = quantize(items, "hid", hid[:], n)
-            acc = last_psum.tile([P, n], F32, name="acc")
-            nc.tensor.matmul_mx(
-                out=acc[:],
-                lhsT=w3_codes[:].bitcast(FP8X4),
-                lhsT_scale=w3_scales[:],
-                rhs=hid_codes[:].bitcast(FP8X4),
-                rhs_scale=hid_scales[:],
-                start=True,
-                stop=True,
-            )
-            result = items.tile([P, n], F32, name="result")
-            nc.scalar.activation(result[:], acc[:], COPY)
-            nc.sync.dma_start(out[:, r0 : r0 + n], result[:])
+        def labels(hid, items):
+            hid_mx = quantize(pieces, "hid", hid[:], width(items))
+            bank = multiply(last_psum, w3_mx, first, hid_mx, slice(0, width(items)))
+            result = pieces.tile([P, width(items)], F32, name="result")
+            nc.scalar.activation(result[:], bank[:], COPY)
+            nc.sync.dma_start(out[:, items], result[:])
 
-        hid = round_hid(*PARTS[0])
-        for i, part in enumerate(PARTS):
-            ahead = round_hid(*PARTS[i + 1]) if i + 1 < len(PARTS) else None
-            labels(hid, *part)
-            hid = ahead
+        for both in (LABEL_PIECES[:2], LABEL_PIECES[2:]):
+            for hid, items in [(round_hid(items), items) for items in both]:
+                labels(hid, items)

from contextlib import ExitStack

import concourse.mybir as mybir

K, T, S, N, H, U = 512, 1024, 512, 128, 512, 1024
FLOPS = 2 * K * H * S * 2 + 2 * H * N * U

F32 = mybir.dt.float32
BF16 = mybir.dt.bfloat16
I32 = mybir.dt.int32
U32 = mybir.dt.uint32
U16 = mybir.dt.uint16
U8 = mybir.dt.uint8
FP8X4 = mybir.dt.float8_e4m3fn_x4
ADD, MULT = mybir.AluOpType.add, mybir.AluOpType.mult
COPY = mybir.ActivationFunctionType.Copy

P = 128
PACK = 4
LANES = 16
QUADRANT = 32

WINDOW = U + LANES

ALL_ITEMS = slice(0, U)
HALVES = (slice(0, U // 2), slice(U // 2, U))
OPENING = (slice(0, U // 4), slice(U // 4, U))
OWN_PIECES = (slice(0, U // 2), slice(U // 2, 3 * U // 4), slice(3 * U // 4, U))
LABEL_PIECES = OWN_PIECES[:2] + (slice(3 * U // 4, 7 * U // 8), slice(7 * U // 8, U))


def tile_picked_yvotepr_tru_p_kernel(tc, x_words, x_scales, w1, w2, unit, w3, offs, va, vb, vc, tr, out):
    nc = tc.nc
    with ExitStack() as ctx:
        lists = ctx.enter_context(tc.tile_pool(name="lists", bufs=1))
        keep = ctx.enter_context(tc.tile_pool(name="keep", bufs=1))
        pieces = ctx.enter_context(tc.tile_pool(name="pieces", bufs=len(LABEL_PIECES)))
        first_psum = ctx.enter_context(tc.psum_pool(name="first_psum", bufs=PACK))
        last_psum = ctx.enter_context(tc.psum_pool(name="last_psum", bufs=len(LABEL_PIECES)))

        def row_tiles(name, width):
            return [keep.tile([P, width], F32, name="%s%d" % (name, t)) for t in range(PACK)]

        def load_list(name, src):
            tile = lists.tile([P, src.shape[1]], U16, name=name)
            nc.sync.dma_start(tile[:], src)
            return tile

        def load_rows(name, w):
            raw = keep.tile([P, PACK, w.shape[1]], F32, name=name)
            nc.sync.dma_start(raw[:], w.rearrange("(p j) c -> p j c", j=PACK))
            return raw

        def width(items):
            return items.stop - items.start

        def entries(offsets, items):
            return offsets[:, items.start // LANES : items.stop // LANES]

        table_scales = keep.tile([P, T], U8, name="table_scales")
        nc.gpsimd.memset(table_scales[:].bitcast(I32), 0)
        unit_sb = keep.tile([P, PACK], F32, name="unit_sb")
        nc.gpsimd.dma_start(unit_sb[:], unit.rearrange("(p t) o -> p (t o)", t=PACK))
        y_win, z_win = row_tiles("y_win", WINDOW), row_tiles("z_win", WINDOW)
        for t in range(PACK):
            nc.vector.memset(y_win[t][:, S:], 0.0)
            nc.gpsimd.memset(z_win[t][:, S:], 0.0)

        offs_sb = load_list("offs_sb", offs)
        table_words = keep.tile([P, T], I32, name="table_words")
        nc.sync.dma_start(table_words[:], x_words[0].rearrange("p n j -> p (n j)").bitcast(I32))
        for q in range(P // QUADRANT):
            nc.sync.dma_start(
                table_scales[QUADRANT * q : QUADRANT * q + PACK, :].bitcast(I32),
                x_scales[0, PACK * q : PACK * (q + 1), :].bitcast(I32),
            )
        w1_left, w1_right = load_rows("w1_left", w1[:, : H // 2]), load_rows("w1_right", w1[:, H // 2 :])
        va_sb = load_list("va_sb", va)
        w2_raw = load_rows("w2_raw", w2)
        vb_sb = load_list("vb_sb", vb)
        vc_sb = load_list("vc_sb", vc)
        tr_sb = load_list("tr_sb", tr)
        w3_raw = load_rows("w3_raw", w3)

        x_codes = keep.tile([P, S], U32, name="x_codes", align_bytes=64)
        x_bytes = keep.tile([P, S], U8, name="x_bytes", align_bytes=64)
        nc.vector.tensor_copy(x_codes[:], table_words[:].bitcast(U32).indirect(offs_sb[:]))
        nc.vector.tensor_copy(x_bytes[:], table_scales[:].indirect(offs_sb[:]))

        def round_pair(copy, rounded, raw, pair, m0):
            copy(
                rounded[:].rearrange("p (e m j) -> p m j e", e=2, j=PACK)[:, m0 : m0 + raw.shape[2] // PACK],
                raw[:].rearrange("p j (m t) -> p m j t", t=PACK)[:, :, :, 2 * pair : 2 * pair + 2],
            )

        def quantize(pool, name, rounded, words):
            codes = pool.tile([P, words], U32, name=name + "_codes", align_bytes=64)
            scales = pool.tile([P, words], U8, name=name + "_scales", align_bytes=64)
            nc.vector.quantize_mx(out=codes[:].bitcast(FP8X4), scales=scales[:], in_=rounded)
            return codes, scales

        def multiply(pool, stationary, cols, moving, moving_cols):
            bank = pool.tile([P, width(moving_cols)], F32, name="bank")
            nc.tensor.matmul_mx(
                out=bank[:],
                lhsT=stationary[0][:, cols].bitcast(FP8X4),
                lhsT_scale=stationary[1][:, cols],
                rhs=moving[0][:, moving_cols].bitcast(FP8X4),
                rhs_scale=moving[1][:, moving_cols],
                start=True,
                stop=True,
            )
            return bank

        def project(stationary, cols, picked):
            return multiply(first_psum, stationary, cols, (x_codes, x_bytes), picked)

        first, second = slice(0, P), slice(P, 2 * P)
        w1_bf = [keep.tile([P, 2 * P * PACK], BF16, name="w1_bf%d" % pair, align_bytes=64) for pair in range(2)]
        w2_bf = [keep.tile([P, 2 * P * PACK], BF16, name="w2_bf%d" % pair, align_bytes=64) for pair in range(2)]

        round_pair(nc.scalar.copy, w1_bf[0], w1_left, 0, 0)
        round_pair(nc.scalar.copy, w1_bf[1], w1_left, 1, 0)
        round_pair(nc.vector.tensor_copy, w1_bf[0], w1_right, 0, P // 2)
        round_pair(nc.scalar.copy, w1_bf[1], w1_right, 1, P // 2)
        w1_tile0 = quantize(keep, "w1_tile0", w1_bf[0][:, : P * PACK], P)
        w1_tile1 = quantize(keep, "w1_tile1", w1_bf[0][:, P * PACK :], P)
        w1_pair1 = quantize(keep, "w1_pair1", w1_bf[1][:], 2 * P)
        w1_mx = [(w1_tile0, first), (w1_tile1, first), (w1_pair1, first), (w1_pair1, second)]

        low, high = slice(0, S // 2), slice(S // 2, S)
        nc.scalar.activation(y_win[0][:, low], project(*w1_mx[0], low)[:], COPY, scale=unit_sb[:, 0:1])
        nc.vector.tensor_scalar(y_win[0][:, high], project(*w1_mx[0], high)[:], unit_sb[:, 0:1], None, MULT)

        for pair in range(2):
            round_pair(nc.vector.tensor_copy, w2_bf[pair], w2_raw, pair, 0)
        w2_pairs = [quantize(keep, "w2_pair%d" % pair, w2_bf[pair][:], 2 * P) for pair in range(2)]
        w2_mx = [(w2_pairs[t // 2], (first, second)[t % 2]) for t in range(PACK)]

        vote_a, vote_ab, vote_abc = row_tiles("vote_a", U), row_tiles("vote_ab", U), row_tiles("vote_abc", U)
        judged = keep.tile([P, PACK, U], F32, name="judged")

        def fill(window, weights, scale):
            nc.scalar.activation(window[:, :S], project(*weights, slice(0, S))[:], COPY, scale=scale)

        def gather(dst, t, offsets, items, scale=1.0):
            nc.scalar.activation(dst, y_win[t][:].indirect(entries(offsets, items)), COPY, scale=scale)

        def add_b_fused(t, items):
            nc.vector.tensor_tensor(
                vote_ab[t][:, items], y_win[t][:].indirect(entries(vb_sb, items)), vote_a[t][:, items], ADD
            )

        def add_c(t, items):
            nc.vector.tensor_tensor(
                vote_abc[t][:, items], y_win[t][:].indirect(entries(vc_sb, items)), vote_ab[t][:, items], ADD
            )

        def judge(t, items):
            nc.vector.tensor_tensor(
                judged[:, t, items], z_win[t][:].indirect(entries(tr_sb, items)), vote_abc[t][:, items], MULT
            )

        for items in OPENING:
            gather(vote_a[0][:, items], 0, va_sb, items)
            add_b_fused(0, items)

        w3_bf = keep.tile([P, N * PACK], BF16, name="w3_bf", align_bytes=64)
        nc.vector.tensor_copy(
            w3_bf[:].rearrange("p (c e j) -> p c j e", e=2, j=PACK),
            w3_raw[:].rearrange("p j (c e) -> p c j e", e=2),
        )

        for t in range(1, PACK):
            fill(y_win[t], w1_mx[t], unit_sb[:, t : t + 1])
            gather(vote_a[t][:], t, va_sb, ALL_ITEMS)
            vote_b = keep.tile([P, U], F32, name="vote_b%d" % t)
            gather(vote_b[:], t, vb_sb, ALL_ITEMS)
            fill(z_win[t - 1], w2_mx[t - 1], 1.0)
            add_c(t - 1, ALL_ITEMS)
            nc.vector.tensor_tensor(vote_ab[t][:], vote_b[:], vote_a[t][:], ADD)
            judge(t - 1, ALL_ITEMS)
        last = PACK - 1
        w3_mx = quantize(keep, "w3", w3_bf[:], N)

        vote_c = keep.tile([P, width(HALVES[1])], F32, name="vote_c")
        gather(vote_c[:], last, vc_sb, HALVES[1])
        fill(z_win[last], w2_mx[last], 1.0)
        add_c(last, HALVES[0])
        nc.vector.tensor_tensor(vote_abc[last][:, HALVES[1]], vote_c[:], vote_ab[last][:, HALVES[1]], ADD)
        for items in HALVES:
            judge(last, items)

        own = {}
        for items in OWN_PIECES:
            own[items.start] = keep.tile([P, PACK, width(items)], F32, name="own%d" % items.start)
            for t in range(PACK):
                gather(own[items.start][:, t, :], t, tr_sb, items, scale=0.5)

        def round_hid(items):
            own_start = max(start for start in own if start <= items.start)
            hid = pieces.tile([P, width(items) * PACK], BF16, name="hid", align_bytes=64)
            nc.vector.tensor_tensor(
                hid[:].rearrange("p (c e t) -> p c t e", e=2, t=PACK),
                judged[:, :, items].rearrange("p t (c e) -> p c t e", e=2),
                own[own_start][:, :, items.start - own_start : items.stop - own_start].rearrange(
                    "p t (c e) -> p c t e", e=2
                ),
                ADD,
            )
            return hid

        def labels(hid, items):
            hid_mx = quantize(pieces, "hid", hid[:], width(items))
            bank = multiply(last_psum, w3_mx, first, hid_mx, slice(0, width(items)))
            result = pieces.tile([P, width(items)], F32, name="result")
            nc.scalar.activation(result[:], bank[:], COPY)
            nc.sync.dma_start(out[:, items], result[:])

        for both in (LABEL_PIECES[:2], LABEL_PIECES[2:]):
            for hid, items in [(round_hid(items), items) for items in both]:
                labels(hid, items)
